import numpy as np
import ml_dtypes


def mxq(x, axis, fmt="e4m3"):
    dtype, down = {"e4m3": (ml_dtypes.float8_e4m3fn, 7), "e5m2": (ml_dtypes.float8_e5m2, 14)}[fmt]
    v = np.moveaxis(np.asarray(x, np.float32).astype(ml_dtypes.bfloat16).astype(np.float64), axis, -1)
    blocks = v.reshape(v.shape[:-1] + (-1, 32))
    amax = np.abs(blocks).max(-1, keepdims=True)
    byte = np.maximum(np.where(amax > 0, np.frexp(amax)[1] - 1 + 127, 0) - down, 1)
    scale = np.exp2(byte - 127.0)
    codes = (blocks / scale).astype(np.float32).astype(dtype).astype(np.float64)
    return np.moveaxis((codes * scale).reshape(v.shape), -1, axis)


WIDE = False


def mx_kscale(k):
    if not WIDE:
        return np.ones(k)
    levels = np.array([10, -10, 5, -5, 0])
    if k % 512:
        return np.exp2(np.random.permutation(np.resize(levels, k // 32))).repeat(32)
    a = np.empty((k // 512, 16))
    for p in range(k // 512):
        a[p, :8] = np.random.permutation(np.resize(levels, 8))
        for g in range(8):
            far = levels[np.abs(levels - a[p, g]) >= 10]
            a[p, g + 8] = far[np.random.randint(len(far))]
    return np.exp2(a.ravel()).repeat(32)


def f64(x):
    return np.asarray(x).astype(np.float64)


def striped(idx):
    return np.tile(idx.reshape(-1, 16).T, (8, 1)).astype(np.uint16)


def unstriped(offs):
    return offs[:16].T.reshape(-1).astype(np.int64)


def relu(v):
    return np.maximum(v, 0.0)


K, T, S, H, N = 512, 2048, 768, 1024, 512


def setup_inputs():
    n = np.random.standard_normal
    s = mx_kscale(K)[:, None]
    u = mx_kscale(H)
    return {
        "xT": (n((K, T)) * s).astype(np.float32),
        "w1": (n((K, H)) / np.sqrt(K) / s * u).astype(np.float32),
        "w2": (n((H, N)) / np.sqrt(H) / u[:, None]).astype(np.float32),
        "offs": striped(np.sort(np.random.permutation(T)[:S])),
    }


def reference(xT, w1, w2, offs):
    idx = unstriped(offs)
    xq = mxq(f64(xT)[:, idx], 0, "e4m3")
    h = relu(mxq(f64(w1), 0, "e4m3").T @ xq)
    y = mxq(f64(w2), 0, "e4m3").T @ mxq(h, 0, "e4m3")
    return y

@@ -1,0 +1,197 @@
+from contextlib import ExitStack
+
+import concourse.mybir as mybir
+
+K, T, S, H, N = 512, 2048, 768, 1024, 512
+P = 128
+PACK = 4
+FLOPS = 2 * S * K * H + 2 * S * H * N
+
+F32 = mybir.dt.float32
+BF16 = mybir.dt.bfloat16
+U32 = mybir.dt.uint32
+U16 = mybir.dt.uint16
+U8 = mybir.dt.uint8
+FP8X4 = mybir.dt.float8_e4m3fn_x4
+RELU = mybir.ActivationFunctionType.Relu
+
+CHUNKS = [(0, 512), (512, 1024), (1024, 1536), (1536, 1792), (1792, 2048)]
+PIECE = 256
+PIECES = S // PIECE
+BLOCK = 128
+
+
+def tile_picked_pick_mlp_relu_srt_e_kernel(tc, xT, w1, w2, offs, out):
+    nc = tc.nc
+    with ExitStack() as ctx:
+        held = ctx.enter_context(tc.tile_pool(name="held", bufs=1))
+        psum = ctx.enter_context(tc.psum_pool(name="psum", bufs=8))
+
+        offsets = held.tile([P, S // 16], U16, name="offsets")
+        raw_x = [held.tile([P, PACK, hi - lo], F32, name=f"raw_x{c}") for c, (lo, hi) in enumerate(CHUNKS)]
+        raw_w1 = [held.tile([P, PACK, 512], F32, name=f"raw_w1_{g}") for g in range(2)]
+        raw_w2 = [held.tile([P, 2, PACK, 256], F32, name=f"raw_w2_{m}") for m in range(2)]
+
+        def load_x(c):
+            lo, hi = CHUNKS[c]
+            nc.sync.dma_start(raw_x[c][:], xT[:, lo:hi].rearrange("(p j) w -> p j w", j=PACK))
+
+        def load_w1(g):
+            nc.sync.dma_start(raw_w1[g][:], w1[:, 512 * g : 512 * (g + 1)].rearrange("(p j) w -> p j w", j=PACK))
+
+        def load_w2(m):
+            for g in range(2):
+                nc.sync.dma_start(
+                    raw_w2[m][:, g],
+                    w2[512 * g : 512 * (g + 1), 256 * m : 256 * (m + 1)].rearrange("(p j) w -> p j w", j=PACK),
+                )
+
+        load_x(0)
+        nc.sync.dma_start(offsets[:], offs)
+        load_x(1)
+        load_x(2)
+        load_w1(0)
+        load_x(3)
+        load_x(4)
+        load_w1(1)
+        load_w2(0)
+        load_w2(1)
+
+        warm = held.tile([P, 1], F32, name="warm")
+        warm_out = held.tile([P, 1], F32, name="warm_out")
+        nc.vector.memset(warm[:], 0.0)
+        nc.scalar.activation(warm_out[:], warm[:], RELU)
+
+        pairs = held.tile([P, 2, 2 * T], BF16, name="pairs", align_bytes=64)
+        picked = [held.tile([P, PACK * PIECE], BF16, name=f"picked{s}", align_bytes=64) for s in range(PIECES)]
+        x_codes = [held.tile([P, PIECE], U32, name=f"x_codes{s}", align_bytes=64) for s in range(PIECES)]
+        x_scales = [held.tile([P, PIECE], U8, name=f"x_scales{s}", align_bytes=64) for s in range(PIECES)]
+        w1_bf = [held.tile([P, 4 * 128 * PACK], BF16, name=f"w1_bf{g}", align_bytes=64) for g in range(2)]
+        w1_codes = [held.tile([P, 512], U32, name=f"w1_codes{g}", align_bytes=64) for g in range(2)]
+        w1_scales = [held.tile([P, 512], U8, name=f"w1_scales{g}", align_bytes=64) for g in range(2)]
+        w2_bf = [held.tile([P, 2, 256 * PACK], BF16, name=f"w2_bf{m}", align_bytes=64) for m in range(2)]
+        w2_codes = [held.tile([P, 512], U32, name=f"w2_codes{m}", align_bytes=64) for m in range(2)]
+        w2_scales = [held.tile([P, 512], U8, name=f"w2_scales{m}", align_bytes=64) for m in range(2)]
+        h_bf = [[held.tile([P, PIECE * PACK], BF16, name=f"h_bf{g}{s}", align_bytes=64) for s in range(PIECES)] for g in range(2)]
+        h_codes = [[held.tile([P, PIECE], U32, name=f"h_codes{g}{s}", align_bytes=64) for s in range(PIECES)] for g in range(2)]
+        h_scales = [[held.tile([P, PIECE], U8, name=f"h_scales{g}{s}", align_bytes=64) for s in range(PIECES)] for g in range(2)]
+
+        def copy(engine, dst, src):
+            if engine == "S":
+                nc.scalar.copy(dst, src)
+            else:
+                nc.vector.tensor_copy(dst, src)
+
+        def cast_x(engine, c, a, b):
+            lo = CHUNKS[c][0]
+            dst = pairs[:, :, 2 * (lo + a) : 2 * (lo + b)].rearrange("p u (w e) -> p u w e", e=2)
+            src = raw_x[c][:, :, a:b].rearrange("p (u e) w -> p u w e", e=2)
+            copy(engine, dst, src)
+
+        def gather(s):
+            window = T - S + PIECE * (s + 1)
+            words = picked[s][:].bitcast(U32)
+            for u in range(2):
+                nc.vector.tensor_copy(
+                    words[:, u::2],
+                    pairs[:, u, : 2 * window].bitcast(U32).indirect(offsets[:, s * PIECE // 16 : (s + 1) * PIECE // 16]),
+                )
+
+        def quantise(codes, scales, values):
+            nc.vector.quantize_mx(out=codes.bitcast(FP8X4), scales=scales, in_=values)
+
+        def cast_w1(engine, g, a, b):
+            dst = w1_bf[g][:].rearrange("p (t m j) -> p t m j", t=4, j=PACK)[:, :, a:b].rearrange("p t m j -> p m t j")
+            src = raw_w1[g][:].rearrange("p j (m t) -> p m t j", t=4)[:, a:b]
+            copy(engine, dst, src)
+
+        def cast_w2(engine, m, g):
+            dst = w2_bf[m][:, g].rearrange("p (w j) -> p w j", j=PACK)
+            src = raw_w2[m][:, g].rearrange("p j w -> p w j")
+            copy(engine, dst, src)
+
+        def layer1(g, s, engines):
+            for b in range(PIECE // BLOCK):
+                bank = psum.tile([P, PACK, BLOCK], F32, name="bank")
+                for t in range(PACK):
+                    nc.tensor.matmul_mx(
+                        out=bank[:, t, :],
+                        lhsT=w1_codes[g][:, 128 * t : 128 * (t + 1)].bitcast(FP8X4),
+                        lhsT_scale=w1_scales[g][:, 128 * t : 128 * (t + 1)],
+                        rhs=x_codes[s][:, BLOCK * b : BLOCK * (b + 1)].bitcast(FP8X4),
+                        rhs_scale=x_scales[s][:, BLOCK * b : BLOCK * (b + 1)],
+                        start=True,
+                        stop=True,
+                    )
+                dst = h_bf[g][s][:, PACK * BLOCK * b : PACK * BLOCK * (b + 1)].rearrange("p (n t) -> p n t", t=PACK)
+                src = bank[:].rearrange("p t n -> p n t")
+                if engines[b] == "S":
+                    nc.scalar.activation(dst, src, RELU)
+                else:
+                    nc.vector.tensor_scalar_max(dst, src, 0.0)
+
+        def quantise_h(g, s):
+            quantise(h_codes[g][s][:], h_scales[g][s][:], h_bf[g][s][:])
+
+        def layer2(m, s, engine):
+            bank = psum.tile([P, 2, PIECE], F32, name="bank")
+            for q in range(2):
+                for g in range(2):
+                    cols = slice(256 * g + 128 * q, 256 * g + 128 * (q + 1))
+                    nc.tensor.matmul_mx(
+                        out=bank[:, q, :],
+                        lhsT=w2_codes[m][:, cols].bitcast(FP8X4),
+                        lhsT_scale=w2_scales[m][:, cols],
+                        rhs=h_codes[g][s][:].bitcast(FP8X4),
+                        rhs_scale=h_scales[g][s][:],
+                        start=(g == 0),
+                        stop=(g == 1),
+                    )
+            result = held.tile([P, 2, PIECE], F32, name=f"result{m}{s}")
+            copy(engine, result[:], bank[:])
+            rows = out[256 * m : 256 * (m + 1), PIECE * s : PIECE * (s + 1)]
+            nc.sync.dma_start(rows.rearrange("(q p) n -> p q n", p=P), result[:])
+
+        for c in range(3):
+            cast_x("S", c, 0, 256)
+            cast_x("V", c, 256, 512)
+        gather(0)
+        cast_w1("S", 0, 0, 64)
+        cast_w1("V", 0, 64, 128)
+        quantise(x_codes[0][:], x_scales[0][:], picked[0][:])
+        cast_x("S", 3, 0, 128)
+        cast_x("V", 3, 128, 256)
+        quantise(w1_codes[0][:], w1_scales[0][:], w1_bf[0][:])
+        layer1(0, 0, "SS")
+        cast_x("S", 4, 0, 128)
+        cast_x("V", 4, 128, 256)
+        gather(1)
+        quantise(x_codes[1][:], x_scales[1][:], picked[1][:])
+        layer1(0, 1, "SS")
+        gather(2)
+        quantise_h(0, 0)
+        cast_w1("S", 1, 0, 64)
+        cast_w1("V", 1, 64, 128)
+        quantise(x_codes[2][:], x_scales[2][:], picked[2][:])
+        quantise(w1_codes[1][:], w1_scales[1][:], w1_bf[1][:])
+        layer1(1, 0, "SV")
+        layer1(0, 2, "SS")
+        cast_w2("V", 0, 0)
+        cast_w2("S", 0, 1)
+        quantise_h(0, 1)
+        quantise(w2_codes[0][:], w2_scales[0][:], w2_bf[0][:].rearrange("p g w -> p (g w)"))
+        layer1(1, 1, "SS")
+        quantise_h(1, 0)
+        layer2(0, 0, "V")
+        cast_w2("V", 1, 0)
+        cast_w2("V", 1, 1)
+        quantise_h(1, 1)
+        quantise(w2_codes[1][:], w2_scales[1][:], w2_bf[1][:].rearrange("p g w -> p (g w)"))
+        layer1(1, 2, "SS")
+        quantise_h(0, 2)
+        quantise_h(1, 2)
+        layer2(0, 1, "S")
+        layer2(1, 0, "S")
+        layer2(1, 1, "V")
+        layer2(0, 2, "S")
+        layer2(1, 2, "V")

@@ -15,7 +15,7 @@ U8 = mybir.dt.uint8
 FP8X4 = mybir.dt.float8_e4m3fn_x4
 RELU = mybir.ActivationFunctionType.Relu
 
-CHUNKS = [(0, 512), (512, 1024), (1024, 1536), (1536, 1792), (1792, 2048)]
+LAST_PLANE_CUTS = [(0, 1024), (1024, 1536), (1536, 2048)]
 PIECE = 256
 PIECES = S // PIECE
 BLOCK = 128
@@ -28,53 +28,51 @@ def tile_picked_pick_mlp_relu_srt_e_kernel(tc, xT, w1, w2, offs, out):
         psum = ctx.enter_context(tc.psum_pool(name="psum", bufs=8))
 
         offsets = held.tile([P, S // 16], U16, name="offsets")
-        raw_x = [held.tile([P, PACK, hi - lo], F32, name=f"raw_x{c}") for c, (lo, hi) in enumerate(CHUNKS)]
+        planes = [held.tile([P, T], F32, name=f"plane{j}", align_bytes=64) for j in range(PACK)]
         raw_w1 = [held.tile([P, PACK, 512], F32, name=f"raw_w1_{g}") for g in range(2)]
-        raw_w2 = [held.tile([P, 2, PACK, 256], F32, name=f"raw_w2_{m}") for m in range(2)]
+        raw_w2 = [held.tile([P, PACK, 512], F32, name=f"raw_w2_{g}") for g in range(2)]
+        picked = held.tile([P, PACK, S], F32, name="picked", align_bytes=64)
+        x_bf = [held.tile([P, PACK * PIECE], BF16, name=f"x_bf{s}", align_bytes=64) for s in range(PIECES)]
+        x_codes = [held.tile([P, PIECE], U32, name=f"x_codes{s}", align_bytes=64) for s in range(PIECES)]
+        x_scales = [held.tile([P, PIECE], U8, name=f"x_scales{s}", align_bytes=64) for s in range(PIECES)]
+        w1_bf = [held.tile([P, 512 * PACK], BF16, name=f"w1_bf{g}", align_bytes=64) for g in range(2)]
+        w1_codes = [held.tile([P, 512], U32, name=f"w1_codes{g}", align_bytes=64) for g in range(2)]
+        w1_scales = [held.tile([P, 512], U8, name=f"w1_scales{g}", align_bytes=64) for g in range(2)]
+        w2_bf = [held.tile([P, 512 * PACK], BF16, name=f"w2_bf{g}", align_bytes=64) for g in range(2)]
+        w2_codes = [held.tile([P, 512], U32, name=f"w2_codes{g}", align_bytes=64) for g in range(2)]
+        w2_scales = [held.tile([P, 512], U8, name=f"w2_scales{g}", align_bytes=64) for g in range(2)]
+        h_bf = [[held.tile([P, PIECE * PACK], BF16, name=f"h_bf{g}{s}", align_bytes=64) for s in range(PIECES)] for g in range(2)]
+        h_codes = [[held.tile([P, PIECE], U32, name=f"h_codes{g}{s}", align_bytes=64) for s in range(PIECES)] for g in range(2)]
+        h_scales = [[held.tile([P, PIECE], U8, name=f"h_scales{g}{s}", align_bytes=64) for s in range(PIECES)] for g in range(2)]
 
-        def load_x(c):
-            lo, hi = CHUNKS[c]
-            nc.sync.dma_start(raw_x[c][:], xT[:, lo:hi].rearrange("(p j) w -> p j w", j=PACK))
+        x_rows = xT.rearrange("(p j) w -> p j w", j=PACK)
+        w1_rows = w1.rearrange("(p j) c -> p j c", j=PACK)
+        w2_rows = w2.rearrange("(g p j) m -> g p j m", g=2, j=PACK)
+
+        def load_plane(j, lo=0, hi=T):
+            nc.sync.dma_start(planes[j][:, lo:hi], x_rows[:, j, lo:hi])
 
         def load_w1(g):
-            nc.sync.dma_start(raw_w1[g][:], w1[:, 512 * g : 512 * (g + 1)].rearrange("(p j) w -> p j w", j=PACK))
+            nc.sync.dma_start(raw_w1[g][:], w1_rows[:, :, 512 * g : 512 * (g + 1)])
 
-        def load_w2(m):
-            for g in range(2):
-                nc.sync.dma_start(
-                    raw_w2[m][:, g],
-                    w2[512 * g : 512 * (g + 1), 256 * m : 256 * (m + 1)].rearrange("(p j) w -> p j w", j=PACK),
-                )
+        def load_w2(g, lo=0, hi=512):
+            nc.sync.dma_start(raw_w2[g][:, :, lo:hi], w2_rows[g, :, :, lo:hi])
 
-        load_x(0)
+        load_plane(0)
         nc.sync.dma_start(offsets[:], offs)
-        load_x(1)
-        load_x(2)
         load_w1(0)
-        load_x(3)
-        load_x(4)
+        load_plane(1)
+        load_plane(2)
+        for lo, hi in LAST_PLANE_CUTS:
+            load_plane(3, lo, hi)
         load_w1(1)
         load_w2(0)
-        load_w2(1)
-
+        load_w2(1, 0, 256)
+        load_w2(1, 256, 512)
         warm = held.tile([P, 1], F32, name="warm")
         warm_out = held.tile([P, 1], F32, name="warm_out")
         nc.vector.memset(warm[:], 0.0)
         nc.scalar.activation(warm_out[:], warm[:], RELU)
-
-        pairs = held.tile([P, 2, 2 * T], BF16, name="pairs", align_bytes=64)
-        picked = [held.tile([P, PACK * PIECE], BF16, name=f"picked{s}", align_bytes=64) for s in range(PIECES)]
-        x_codes = [held.tile([P, PIECE], U32, name=f"x_codes{s}", align_bytes=64) for s in range(PIECES)]
-        x_scales = [held.tile([P, PIECE], U8, name=f"x_scales{s}", align_bytes=64) for s in range(PIECES)]
-        w1_bf = [held.tile([P, 4 * 128 * PACK], BF16, name=f"w1_bf{g}", align_bytes=64) for g in range(2)]
-        w1_codes = [held.tile([P, 512], U32, name=f"w1_codes{g}", align_bytes=64) for g in range(2)]
-        w1_scales = [held.tile([P, 512], U8, name=f"w1_scales{g}", align_bytes=64) for g in range(2)]
-        w2_bf = [held.tile([P, 2, 256 * PACK], BF16, name=f"w2_bf{m}", align_bytes=64) for m in range(2)]
-        w2_codes = [held.tile([P, 512], U32, name=f"w2_codes{m}", align_bytes=64) for m in range(2)]
-        w2_scales = [held.tile([P, 512], U8, name=f"w2_scales{m}", align_bytes=64) for m in range(2)]
-        h_bf = [[held.tile([P, PIECE * PACK], BF16, name=f"h_bf{g}{s}", align_bytes=64) for s in range(PIECES)] for g in range(2)]
-        h_codes = [[held.tile([P, PIECE], U32, name=f"h_codes{g}{s}", align_bytes=64) for s in range(PIECES)] for g in range(2)]
-        h_scales = [[held.tile([P, PIECE], U8, name=f"h_scales{g}{s}", align_bytes=64) for s in range(PIECES)] for g in range(2)]
 
         def copy(engine, dst, src):
             if engine == "S":
@@ -82,33 +80,42 @@ def tile_picked_pick_mlp_relu_srt_e_kernel(tc, xT, w1, w2, offs, out):
             else:
                 nc.vector.tensor_copy(dst, src)
 
-        def cast_x(engine, c, a, b):
-            lo = CHUNKS[c][0]
-            dst = pairs[:, :, 2 * (lo + a) : 2 * (lo + b)].rearrange("p u (w e) -> p u w e", e=2)
-            src = raw_x[c][:, :, a:b].rearrange("p (u e) w -> p u w e", e=2)
-            copy(engine, dst, src)
+        def gather_plane(j):
+            nc.vector.tensor_copy(picked[:, j, :], planes[j][:].indirect(offsets[:]))
 
-        def gather(s):
+        def gather_last(s):
             window = T - S + PIECE * (s + 1)
-            words = picked[s][:].bitcast(U32)
-            for u in range(2):
-                nc.vector.tensor_copy(
-                    words[:, u::2],
-                    pairs[:, u, : 2 * window].bitcast(U32).indirect(offsets[:, s * PIECE // 16 : (s + 1) * PIECE // 16]),
-                )
+            nc.vector.tensor_copy(
+                picked[:, PACK - 1, PIECE * s : PIECE * (s + 1)],
+                planes[PACK - 1][:, :window].indirect(offsets[:, PIECE * s // 16 : PIECE * (s + 1) // 16]),
+            )
+
+        def cast_x(engine, s, a, b):
+            dst = x_bf[s][:, PACK * a : PACK * b].rearrange("p (c i j) -> p c j i", i=4, j=PACK)
+            src = picked[:, :, PIECE * s + a : PIECE * s + b].rearrange("p j (c i) -> p c j i", i=4)
+            copy(engine, dst, src)
 
         def quantise(codes, scales, values):
             nc.vector.quantize_mx(out=codes.bitcast(FP8X4), scales=scales, in_=values)
 
+        def quantise_x(s):
+            quantise(x_codes[s][:], x_scales[s][:], x_bf[s][:])
+
         def cast_w1(engine, g, a, b):
-            dst = w1_bf[g][:].rearrange("p (t m j) -> p t m j", t=4, j=PACK)[:, :, a:b].rearrange("p t m j -> p m t j")
-            src = raw_w1[g][:].rearrange("p j (m t) -> p m t j", t=4)[:, a:b]
+            dst = w1_bf[g][:].rearrange("p (t m j) -> p m j t", t=4, j=PACK)[:, a:b]
+            src = raw_w1[g][:].rearrange("p j (m t) -> p m j t", t=4)[:, a:b]
             copy(engine, dst, src)
 
-        def cast_w2(engine, m, g):
-            dst = w2_bf[m][:, g].rearrange("p (w j) -> p w j", j=PACK)
-            src = raw_w2[m][:, g].rearrange("p j w -> p w j")
+        def quantise_w1(g):
+            quantise(w1_codes[g][:], w1_scales[g][:], w1_bf[g][:])
+
+        def cast_w2(engine, g, a, b):
+            dst = w2_bf[g][:, PACK * a : PACK * b].rearrange("p (c i j) -> p c j i", i=4, j=PACK)
+            src = raw_w2[g][:, :, a:b].rearrange("p j (c i) -> p c j i", i=4)
             copy(engine, dst, src)
+
+        def quantise_w2(g, a, b):
+            quantise(w2_codes[g][:, a:b], w2_scales[g][:, a:b], w2_bf[g][:, PACK * a : PACK * b])
 
         def layer1(g, s, engines):
             for b in range(PIECE // BLOCK):
@@ -136,12 +143,12 @@ def tile_picked_pick_mlp_relu_srt_e_kernel(tc, xT, w1, w2, offs, out):
         def layer2(m, s, engine):
             bank = psum.tile([P, 2, PIECE], F32, name="bank")
             for q in range(2):
+                cols = slice(256 * m + 128 * q, 256 * m + 128 * (q + 1))
                 for g in range(2):
-                    cols = slice(256 * g + 128 * q, 256 * g + 128 * (q + 1))
                     nc.tensor.matmul_mx(
                         out=bank[:, q, :],
-                        lhsT=w2_codes[m][:, cols].bitcast(FP8X4),
-                        lhsT_scale=w2_scales[m][:, cols],
+                        lhsT=w2_codes[g][:, cols].bitcast(FP8X4),
+                        lhsT_scale=w2_scales[g][:, cols],
                         rhs=h_codes[g][s][:].bitcast(FP8X4),
                         rhs_scale=h_scales[g][s][:],
                         start=(g == 0),
@@ -152,46 +159,48 @@ def tile_picked_pick_mlp_relu_srt_e_kernel(tc, xT, w1, w2, offs, out):
             rows = out[256 * m : 256 * (m + 1), PIECE * s : PIECE * (s + 1)]
             nc.sync.dma_start(rows.rearrange("(q p) n -> p q n", p=P), result[:])
 
-        for c in range(3):
-            cast_x("S", c, 0, 256)
-            cast_x("V", c, 256, 512)
-        gather(0)
-        cast_w1("S", 0, 0, 64)
-        cast_w1("V", 0, 64, 128)
-        quantise(x_codes[0][:], x_scales[0][:], picked[0][:])
-        cast_x("S", 3, 0, 128)
-        cast_x("V", 3, 128, 256)
-        quantise(w1_codes[0][:], w1_scales[0][:], w1_bf[0][:])
+        gather_plane(0)
+        cast_w1("S", 0, 0, 128)
+        quantise_w1(0)
+        gather_plane(1)
+        gather_plane(2)
+        gather_last(0)
+        cast_x("S", 0, 0, 128)
+        cast_x("V", 0, 128, 256)
+        gather_last(1)
+        quantise_x(0)
         layer1(0, 0, "SS")
-        cast_x("S", 4, 0, 128)
-        cast_x("V", 4, 128, 256)
-        gather(1)
-        quantise(x_codes[1][:], x_scales[1][:], picked[1][:])
+        cast_x("S", 1, 0, 128)
+        cast_x("V", 1, 128, 256)
+        gather_last(2)
+        quantise_x(1)
         layer1(0, 1, "SS")
-        gather(2)
+        cast_x("S", 2, 0, 64)
+        cast_x("V", 2, 64, 256)
+        quantise_x(2)
+        cast_w1("S", 1, 0, 32)
+        cast_w1("V", 1, 32, 128)
+        quantise_w1(1)
         quantise_h(0, 0)
-        cast_w1("S", 1, 0, 64)
-        cast_w1("V", 1, 64, 128)
-        quantise(x_codes[2][:], x_scales[2][:], picked[2][:])
-        quantise(w1_codes[1][:], w1_scales[1][:], w1_bf[1][:])
-        layer1(1, 0, "SV")
+        layer1(1, 0, "SS")
         layer1(0, 2, "SS")
-        cast_w2("V", 0, 0)
-        cast_w2("S", 0, 1)
+        cast_w2("S", 0, 0, 128)
+        cast_w2("V", 0, 128, 512)
         quantise_h(0, 1)
-        quantise(w2_codes[0][:], w2_scales[0][:], w2_bf[0][:].rearrange("p g w -> p (g w)"))
-        layer1(1, 1, "SS")
+        quantise_w2(0, 0, 512)
         quantise_h(1, 0)
-        layer2(0, 0, "V")
-        cast_w2("V", 1, 0)
-        cast_w2("V", 1, 1)
+        layer1(1, 1, "SS")
+        cast_w2("V", 1, 0, 256)
+        quantise_w2(1, 0, 256)
+        layer1(1, 2, "SV")
+        cast_w2("V", 1, 256, 512)
         quantise_h(1, 1)
-        quantise(w2_codes[1][:], w2_scales[1][:], w2_bf[1][:].rearrange("p g w -> p (g w)"))
-        layer1(1, 2, "SS")
+        quantise_w2(1, 256, 512)
         quantise_h(0, 2)
-        quantise_h(1, 2)
-        layer2(0, 1, "S")
+        layer2(0, 0, "S")
         layer2(1, 0, "S")
-        layer2(1, 1, "V")
-        layer2(0, 2, "S")
-        layer2(1, 2, "V")
+        quantise_h(1, 2)
+        layer2(0, 1, "V")
+        layer2(1, 1, "S")
+        layer2(0, 2, "V")
+        layer2(1, 2, "S")

@@ -15,7 +15,6 @@ U8 = mybir.dt.uint8
 FP8X4 = mybir.dt.float8_e4m3fn_x4
 RELU = mybir.ActivationFunctionType.Relu
 
-LAST_PLANE_CUTS = [(0, 1024), (1024, 1536), (1536, 2048)]
 PIECE = 256
 PIECES = S // PIECE
 BLOCK = 128
@@ -42,8 +41,8 @@ def tile_picked_pick_mlp_relu_srt_e_kernel(tc, xT, w1, w2, offs, out):
         w2_codes = [held.tile([P, 512], U32, name=f"w2_codes{g}", align_bytes=64) for g in range(2)]
         w2_scales = [held.tile([P, 512], U8, name=f"w2_scales{g}", align_bytes=64) for g in range(2)]
         h_bf = [[held.tile([P, PIECE * PACK], BF16, name=f"h_bf{g}{s}", align_bytes=64) for s in range(PIECES)] for g in range(2)]
-        h_codes = [[held.tile([P, PIECE], U32, name=f"h_codes{g}{s}", align_bytes=64) for s in range(PIECES)] for g in range(2)]
-        h_scales = [[held.tile([P, PIECE], U8, name=f"h_scales{g}{s}", align_bytes=64) for s in range(PIECES)] for g in range(2)]
+        h_codes = [held.tile([P, S], U32, name=f"h_codes{g}", align_bytes=64) for g in range(2)]
+        h_scales = [held.tile([P, S], U8, name=f"h_scales{g}", align_bytes=64) for g in range(2)]
 
         x_rows = xT.rearrange("(p j) w -> p j w", j=PACK)
         w1_rows = w1.rearrange("(p j) c -> p j c", j=PACK)
@@ -52,23 +51,22 @@ def tile_picked_pick_mlp_relu_srt_e_kernel(tc, xT, w1, w2, offs, out):
         def load_plane(j, lo=0, hi=T):
             nc.sync.dma_start(planes[j][:, lo:hi], x_rows[:, j, lo:hi])
 
-        def load_w1(g):
-            nc.sync.dma_start(raw_w1[g][:], w1_rows[:, :, 512 * g : 512 * (g + 1)])
+        def load_w1(g, lo=0, hi=512):
+            nc.sync.dma_start(raw_w1[g][:, :, lo:hi], w1_rows[:, :, 512 * g + lo : 512 * g + hi])
 
         def load_w2(g, lo=0, hi=512):
             nc.sync.dma_start(raw_w2[g][:, :, lo:hi], w2_rows[g, :, :, lo:hi])
 
         load_plane(0)
         nc.sync.dma_start(offsets[:], offs)
-        load_w1(0)
         load_plane(1)
         load_plane(2)
-        for lo, hi in LAST_PLANE_CUTS:
-            load_plane(3, lo, hi)
+        load_plane(3, 0, 1536)
+        load_plane(3, 1536, 2048)
+        load_w1(0)
         load_w1(1)
         load_w2(0)
-        load_w2(1, 0, 256)
-        load_w2(1, 256, 512)
+        load_w2(1)
         warm = held.tile([P, 1], F32, name="warm")
         warm_out = held.tile([P, 1], F32, name="warm_out")
         nc.vector.memset(warm[:], 0.0)
@@ -106,8 +104,8 @@ def tile_picked_pick_mlp_relu_srt_e_kernel(tc, xT, w1, w2, offs, out):
             src = raw_w1[g][:].rearrange("p j (m t) -> p m j t", t=4)[:, a:b]
             copy(engine, dst, src)
 
-        def quantise_w1(g):
-            quantise(w1_codes[g][:], w1_scales[g][:], w1_bf[g][:])
+        def quantise_w1(g, a, b):
+            quantise(w1_codes[g][:, a:b], w1_scales[g][:, a:b], w1_bf[g][:, PACK * a : PACK * b])
 
         def cast_w2(engine, g, a, b):
             dst = w2_bf[g][:, PACK * a : PACK * b].rearrange("p (c i j) -> p c j i", i=4, j=PACK)
@@ -117,90 +115,95 @@ def tile_picked_pick_mlp_relu_srt_e_kernel(tc, xT, w1, w2, offs, out):
         def quantise_w2(g, a, b):
             quantise(w2_codes[g][:, a:b], w2_scales[g][:, a:b], w2_bf[g][:, PACK * a : PACK * b])
 
-        def layer1(g, s, engines):
-            for b in range(PIECE // BLOCK):
-                bank = psum.tile([P, PACK, BLOCK], F32, name="bank")
-                for t in range(PACK):
-                    nc.tensor.matmul_mx(
-                        out=bank[:, t, :],
-                        lhsT=w1_codes[g][:, 128 * t : 128 * (t + 1)].bitcast(FP8X4),
-                        lhsT_scale=w1_scales[g][:, 128 * t : 128 * (t + 1)],
-                        rhs=x_codes[s][:, BLOCK * b : BLOCK * (b + 1)].bitcast(FP8X4),
-                        rhs_scale=x_scales[s][:, BLOCK * b : BLOCK * (b + 1)],
-                        start=True,
-                        stop=True,
-                    )
-                dst = h_bf[g][s][:, PACK * BLOCK * b : PACK * BLOCK * (b + 1)].rearrange("p (n t) -> p n t", t=PACK)
-                src = bank[:].rearrange("p t n -> p n t")
-                if engines[b] == "S":
-                    nc.scalar.activation(dst, src, RELU)
-                else:
-                    nc.vector.tensor_scalar_max(dst, src, 0.0)
+        def layer1(g, s, b, engine):
+            bank = psum.tile([P, PACK, BLOCK], F32, name="bank")
+            for t in range(PACK):
+                nc.tensor.matmul_mx(
+                    out=bank[:, t, :],
+                    lhsT=w1_codes[g][:, 128 * t : 128 * (t + 1)].bitcast(FP8X4),
+                    lhsT_scale=w1_scales[g][:, 128 * t : 128 * (t + 1)],
+                    rhs=x_codes[s][:, BLOCK * b : BLOCK * (b + 1)].bitcast(FP8X4),
+                    rhs_scale=x_scales[s][:, BLOCK * b : BLOCK * (b + 1)],
+                    start=True,
+                    stop=True,
+                )
+            dst = h_bf[g][s][:, PACK * BLOCK * b : PACK * BLOCK * (b + 1)].rearrange("p (n t) -> p n t", t=PACK)
+            src = bank[:].rearrange("p t n -> p n t")
+            if engine == "S":
+                nc.scalar.activation(dst, src, RELU)
+            else:
+                nc.vector.tensor_scalar_max(dst, src, 0.0)
 
         def quantise_h(g, s):
-            quantise(h_codes[g][s][:], h_scales[g][s][:], h_bf[g][s][:])
+            cols = slice(PIECE * s, PIECE * (s + 1))
+            quantise(h_codes[g][:, cols], h_scales[g][:, cols], h_bf[g][s][:])
 
-        def layer2(m, s, engine):
-            bank = psum.tile([P, 2, PIECE], F32, name="bank")
-            for q in range(2):
-                cols = slice(256 * m + 128 * q, 256 * m + 128 * (q + 1))
-                for g in range(2):
-                    nc.tensor.matmul_mx(
-                        out=bank[:, q, :],
-                        lhsT=w2_codes[g][:, cols].bitcast(FP8X4),
-                        lhsT_scale=w2_scales[g][:, cols],
-                        rhs=h_codes[g][s][:].bitcast(FP8X4),
-                        rhs_scale=h_scales[g][s][:],
-                        start=(g == 0),
-                        stop=(g == 1),
-                    )
-            result = held.tile([P, 2, PIECE], F32, name=f"result{m}{s}")
+        def layer2(m, lo, hi, engine):
+            bank = psum.tile([P, hi - lo], F32, name="bank")
+            rows = slice(P * m, P * (m + 1))
+            for g in range(2):
+                nc.tensor.matmul_mx(
+                    out=bank[:],
+                    lhsT=w2_codes[g][:, rows].bitcast(FP8X4),
+                    lhsT_scale=w2_scales[g][:, rows],
+                    rhs=h_codes[g][:, lo:hi].bitcast(FP8X4),
+                    rhs_scale=h_scales[g][:, lo:hi],
+                    start=(g == 0),
+                    stop=(g == 1),
+                )
+            result = held.tile([P, hi - lo], F32, name=f"result{m}_{lo}")
             copy(engine, result[:], bank[:])
-            rows = out[256 * m : 256 * (m + 1), PIECE * s : PIECE * (s + 1)]
-            nc.sync.dma_start(rows.rearrange("(q p) n -> p q n", p=P), result[:])
+            nc.sync.dma_start(out[rows, lo:hi], result[:])
 
+        cast_w1("V", 0, 0, 96)
         gather_plane(0)
-        cast_w1("S", 0, 0, 128)
-        quantise_w1(0)
         gather_plane(1)
         gather_plane(2)
-        gather_last(0)
-        cast_x("S", 0, 0, 128)
-        cast_x("V", 0, 128, 256)
         gather_last(1)
+        cast_w1("S", 0, 96, 128)
+        cast_w1("S", 1, 80, 128)
+        gather_last(0)
+        cast_x("V", 0, 0, 160)
+        cast_x("S", 1, 0, 256)
+        cast_x("S", 0, 160, 256)
         quantise_x(0)
-        layer1(0, 0, "SS")
-        cast_x("S", 1, 0, 128)
-        cast_x("V", 1, 128, 256)
+        quantise_w1(0, 256, 512)
+        quantise_w1(0, 0, 256)
         gather_last(2)
-        quantise_x(1)
-        layer1(0, 1, "SS")
-        cast_x("S", 2, 0, 64)
-        cast_x("V", 2, 64, 256)
+        cast_x("V", 2, 0, 256)
+        layer1(0, 0, 0, "S")
         quantise_x(2)
-        cast_w1("S", 1, 0, 32)
-        cast_w1("V", 1, 32, 128)
-        quantise_w1(1)
+        quantise_x(1)
+        layer1(0, 1, 0, "S")
+        layer1(0, 2, 1, "V")
+        cast_w1("V", 1, 0, 80)
+        quantise_w1(1, 0, 512)
+        layer1(1, 0, 0, "S")
+        layer1(0, 0, 1, "S")
+        layer1(1, 1, 1, "S")
         quantise_h(0, 0)
-        layer1(1, 0, "SS")
-        layer1(0, 2, "SS")
-        cast_w2("S", 0, 0, 128)
-        cast_w2("V", 0, 128, 512)
+        layer1(1, 0, 1, "S")
+        layer1(1, 1, 0, "S")
+        layer1(0, 1, 1, "S")
+        layer1(1, 2, 1, "S")
         quantise_h(0, 1)
-        quantise_w2(0, 0, 512)
         quantise_h(1, 0)
-        layer1(1, 1, "SS")
+        cast_w2("V", 0, 0, 512)
+        quantise_w2(0, 0, 512)
+        layer1(1, 2, 0, "S")
         cast_w2("V", 1, 0, 256)
+        layer1(0, 2, 0, "S")
         quantise_w2(1, 0, 256)
-        layer1(1, 2, "SV")
-        cast_w2("V", 1, 256, 512)
-        quantise_h(1, 1)
-        quantise_w2(1, 256, 512)
         quantise_h(0, 2)
-        layer2(0, 0, "S")
-        layer2(1, 0, "S")
+        quantise_h(1, 1)
+        layer2(0, 0, 512, "S")
+        cast_w2("V", 1, 256, 512)
+        layer2(1, 0, 512, "S")
+        quantise_w2(1, 256, 512)
         quantise_h(1, 2)
-        layer2(0, 1, "V")
-        layer2(1, 1, "S")
-        layer2(0, 2, "V")
-        layer2(1, 2, "S")
+        layer2(2, 0, 512, "V")
+        layer2(3, 0, 512, "S")
+        layer2(0, 512, 768, "V")
+        layer2(1, 512, 768, "S")
+        layer2(2, 512, 768, "V")
+        layer2(3, 512, 768, "S")

@@ -3,9 +3,16 @@ from contextlib import ExitStack
 import concourse.mybir as mybir
 
 K, T, S, H, N = 512, 2048, 768, 1024, 512
+FLOPS = 2 * S * K * H + 2 * S * H * N
+
 P = 128
 PACK = 4
-FLOPS = 2 * S * K * H + 2 * S * H * N
+HALF = P * PACK
+HALVES = H // HALF
+PIECE = 256
+PIECES = S // PIECE
+BLOCK = 128
+WIDE = 2 * PIECE
 
 F32 = mybir.dt.float32
 BF16 = mybir.dt.bfloat16
@@ -15,10 +22,6 @@ U8 = mybir.dt.uint8
 FP8X4 = mybir.dt.float8_e4m3fn_x4
 RELU = mybir.ActivationFunctionType.Relu
 
-PIECE = 256
-PIECES = S // PIECE
-BLOCK = 128
-
 
 def tile_picked_pick_mlp_relu_srt_e_kernel(tc, xT, w1, w2, offs, out):
     nc = tc.nc
@@ -26,122 +29,127 @@ def tile_picked_pick_mlp_relu_srt_e_kernel(tc, xT, w1, w2, offs, out):
         held = ctx.enter_context(tc.tile_pool(name="held", bufs=1))
         psum = ctx.enter_context(tc.psum_pool(name="psum", bufs=8))
 
+        def words(width, name):
+            return held.tile([P, width], U32, name=name, align_bytes=64)
+
+        def scale_bytes(width, name):
+            return held.tile([P, width], U8, name=name, align_bytes=64)
+
+        def bf16_values(width, name):
+            return held.tile([P, PACK * width], BF16, name=name, align_bytes=64)
+
         offsets = held.tile([P, S // 16], U16, name="offsets")
         planes = [held.tile([P, T], F32, name=f"plane{j}", align_bytes=64) for j in range(PACK)]
-        raw_w1 = [held.tile([P, PACK, 512], F32, name=f"raw_w1_{g}") for g in range(2)]
-        raw_w2 = [held.tile([P, PACK, 512], F32, name=f"raw_w2_{g}") for g in range(2)]
         picked = held.tile([P, PACK, S], F32, name="picked", align_bytes=64)
-        x_bf = [held.tile([P, PACK * PIECE], BF16, name=f"x_bf{s}", align_bytes=64) for s in range(PIECES)]
-        x_codes = [held.tile([P, PIECE], U32, name=f"x_codes{s}", align_bytes=64) for s in range(PIECES)]
-        x_scales = [held.tile([P, PIECE], U8, name=f"x_scales{s}", align_bytes=64) for s in range(PIECES)]
-        w1_bf = [held.tile([P, 512 * PACK], BF16, name=f"w1_bf{g}", align_bytes=64) for g in range(2)]
-        w1_codes = [held.tile([P, 512], U32, name=f"w1_codes{g}", align_bytes=64) for g in range(2)]
-        w1_scales = [held.tile([P, 512], U8, name=f"w1_scales{g}", align_bytes=64) for g in range(2)]
-        w2_bf = [held.tile([P, 512 * PACK], BF16, name=f"w2_bf{g}", align_bytes=64) for g in range(2)]
-        w2_codes = [held.tile([P, 512], U32, name=f"w2_codes{g}", align_bytes=64) for g in range(2)]
-        w2_scales = [held.tile([P, 512], U8, name=f"w2_scales{g}", align_bytes=64) for g in range(2)]
-        h_bf = [[held.tile([P, PIECE * PACK], BF16, name=f"h_bf{g}{s}", align_bytes=64) for s in range(PIECES)] for g in range(2)]
-        h_codes = [held.tile([P, S], U32, name=f"h_codes{g}", align_bytes=64) for g in range(2)]
-        h_scales = [held.tile([P, S], U8, name=f"h_scales{g}", align_bytes=64) for g in range(2)]
+        raw_w1 = [held.tile([P, PACK, HALF], F32, name=f"raw_w1_{g}") for g in range(HALVES)]
+        raw_w2 = [held.tile([P, PACK, N], F32, name=f"raw_w2_{g}") for g in range(HALVES)]
+        x_bf = [bf16_values(PIECE, f"x_bf{s}") for s in range(PIECES)]
+        x_codes = [words(PIECE, f"x_codes{s}") for s in range(PIECES)]
+        x_scales = [scale_bytes(PIECE, f"x_scales{s}") for s in range(PIECES)]
+        w1_bf = [bf16_values(HALF, f"w1_bf{g}") for g in range(HALVES)]
+        w1_codes = [words(HALF, f"w1_codes{g}") for g in range(HALVES)]
+        w1_scales = [scale_bytes(HALF, f"w1_scales{g}") for g in range(HALVES)]
+        w2_bf = [bf16_values(N, f"w2_bf{g}") for g in range(HALVES)]
+        w2_codes = [words(N, f"w2_codes{g}") for g in range(HALVES)]
+        w2_scales = [scale_bytes(N, f"w2_scales{g}") for g in range(HALVES)]
+        h_bf = [[bf16_values(PIECE, f"h_bf{g}{s}") for s in range(PIECES)] for g in range(HALVES)]
+        h_codes = [words(S, f"h_codes{g}") for g in range(HALVES)]
+        h_scales = [scale_bytes(S, f"h_scales{g}") for g in range(HALVES)]
 
         x_rows = xT.rearrange("(p j) w -> p j w", j=PACK)
-        w1_rows = w1.rearrange("(p j) c -> p j c", j=PACK)
-        w2_rows = w2.rearrange("(g p j) m -> g p j m", g=2, j=PACK)
-
-        def load_plane(j, lo=0, hi=T):
-            nc.sync.dma_start(planes[j][:, lo:hi], x_rows[:, j, lo:hi])
-
-        def load_w1(g, lo=0, hi=512):
-            nc.sync.dma_start(raw_w1[g][:, :, lo:hi], w1_rows[:, :, 512 * g + lo : 512 * g + hi])
-
-        def load_w2(g, lo=0, hi=512):
-            nc.sync.dma_start(raw_w2[g][:, :, lo:hi], w2_rows[g, :, :, lo:hi])
-
-        load_plane(0)
+        w1_rows = w1.rearrange("(p j) i -> p j i", j=PACK)
+        w2_rows = w2.rearrange("(g p j) m -> g p j m", g=HALVES, j=PACK)
+        first_part = T - S + PIECE
+        nc.sync.dma_start(planes[0][:], x_rows[:, 0, :])
         nc.sync.dma_start(offsets[:], offs)
-        load_plane(1)
-        load_plane(2)
-        load_plane(3, 0, 1536)
-        load_plane(3, 1536, 2048)
-        load_w1(0)
-        load_w1(1)
-        load_w2(0)
-        load_w2(1)
-        warm = held.tile([P, 1], F32, name="warm")
+        nc.sync.dma_start(planes[1][:], x_rows[:, 1, :])
+        nc.sync.dma_start(planes[2][:], x_rows[:, 2, :])
+        nc.sync.dma_start(planes[3][:, :first_part], x_rows[:, 3, :first_part])
+        nc.sync.dma_start(planes[3][:, first_part:], x_rows[:, 3, first_part:])
+        for g in range(HALVES):
+            nc.sync.dma_start(raw_w1[g][:], w1_rows[:, :, HALF * g : HALF * (g + 1)])
+        for g in range(HALVES):
+            nc.sync.dma_start(raw_w2[g][:], w2_rows[g])
+
+        warm_in = held.tile([P, 1], F32, name="warm_in")
         warm_out = held.tile([P, 1], F32, name="warm_out")
-        nc.vector.memset(warm[:], 0.0)
-        nc.scalar.activation(warm_out[:], warm[:], RELU)
+        nc.vector.memset(warm_in[:], 0.0)
+        nc.scalar.activation(warm_out[:], warm_in[:], RELU)
 
         def copy(engine, dst, src):
-            if engine == "S":
+            if engine == "scalar":
                 nc.scalar.copy(dst, src)
             else:
                 nc.vector.tensor_copy(dst, src)
 
+        def quantise(codes, scales, values):
+            nc.vector.quantize_mx(out=codes.bitcast(FP8X4), scales=scales, in_=values)
+
         def gather_plane(j):
             nc.vector.tensor_copy(picked[:, j, :], planes[j][:].indirect(offsets[:]))
 
-        def gather_last(s):
+        def gather_last_plane(s):
+            entries = slice(PIECE * s, PIECE * (s + 1))
             window = T - S + PIECE * (s + 1)
             nc.vector.tensor_copy(
-                picked[:, PACK - 1, PIECE * s : PIECE * (s + 1)],
+                picked[:, PACK - 1, entries],
                 planes[PACK - 1][:, :window].indirect(offsets[:, PIECE * s // 16 : PIECE * (s + 1) // 16]),
             )
 
-        def cast_x(engine, s, a, b):
-            dst = x_bf[s][:, PACK * a : PACK * b].rearrange("p (c i j) -> p c j i", i=4, j=PACK)
-            src = picked[:, :, PIECE * s + a : PIECE * s + b].rearrange("p j (c i) -> p c j i", i=4)
-            copy(engine, dst, src)
+        def interleave(engine, dst, src):
+            copy(
+                engine,
+                dst.rearrange("p (q c j) -> p q j c", c=4, j=PACK),
+                src.rearrange("p j (q c) -> p q j c", c=4),
+            )
 
-        def quantise(codes, scales, values):
-            nc.vector.quantize_mx(out=codes.bitcast(FP8X4), scales=scales, in_=values)
+        def interleave_x(engine, s, lo, hi):
+            interleave(engine, x_bf[s][:, PACK * lo : PACK * hi], picked[:, :, PIECE * s + lo : PIECE * s + hi])
 
         def quantise_x(s):
             quantise(x_codes[s][:], x_scales[s][:], x_bf[s][:])
 
-        def cast_w1(engine, g, a, b):
-            dst = w1_bf[g][:].rearrange("p (t m j) -> p m j t", t=4, j=PACK)[:, a:b]
-            src = raw_w1[g][:].rearrange("p j (m t) -> p m j t", t=4)[:, a:b]
-            copy(engine, dst, src)
+        def interleave_w1(engine, g, lo, hi):
+            dst = w1_bf[g][:].rearrange("p (t m j) -> p m j t", t=PACK, j=PACK)
+            src = raw_w1[g][:].rearrange("p j (m t) -> p m j t", t=PACK)
+            copy(engine, dst[:, lo:hi], src[:, lo:hi])
 
-        def quantise_w1(g, a, b):
-            quantise(w1_codes[g][:, a:b], w1_scales[g][:, a:b], w1_bf[g][:, PACK * a : PACK * b])
+        def quantise_w1(g, lo, hi):
+            quantise(w1_codes[g][:, lo:hi], w1_scales[g][:, lo:hi], w1_bf[g][:, PACK * lo : PACK * hi])
 
-        def cast_w2(engine, g, a, b):
-            dst = w2_bf[g][:, PACK * a : PACK * b].rearrange("p (c i j) -> p c j i", i=4, j=PACK)
-            src = raw_w2[g][:, :, a:b].rearrange("p j (c i) -> p c j i", i=4)
-            copy(engine, dst, src)
+        def interleave_w2(engine, g, lo, hi):
+            interleave(engine, w2_bf[g][:, PACK * lo : PACK * hi], raw_w2[g][:, :, lo:hi])
 
-        def quantise_w2(g, a, b):
-            quantise(w2_codes[g][:, a:b], w2_scales[g][:, a:b], w2_bf[g][:, PACK * a : PACK * b])
+        def quantise_w2(g, lo, hi):
+            quantise(w2_codes[g][:, lo:hi], w2_scales[g][:, lo:hi], w2_bf[g][:, PACK * lo : PACK * hi])
 
-        def layer1(g, s, b, engine):
+        def layer1(g, s, b):
             bank = psum.tile([P, PACK, BLOCK], F32, name="bank")
+            tokens = slice(BLOCK * b, BLOCK * (b + 1))
             for t in range(PACK):
+                channels = slice(P * t, P * (t + 1))
                 nc.tensor.matmul_mx(
                     out=bank[:, t, :],
-                    lhsT=w1_codes[g][:, 128 * t : 128 * (t + 1)].bitcast(FP8X4),
-                    lhsT_scale=w1_scales[g][:, 128 * t : 128 * (t + 1)],
-                    rhs=x_codes[s][:, BLOCK * b : BLOCK * (b + 1)].bitcast(FP8X4),
-                    rhs_scale=x_scales[s][:, BLOCK * b : BLOCK * (b + 1)],
+                    lhsT=w1_codes[g][:, channels].bitcast(FP8X4),
+                    lhsT_scale=w1_scales[g][:, channels],
+                    rhs=x_codes[s][:, tokens].bitcast(FP8X4),
+                    rhs_scale=x_scales[s][:, tokens],
                     start=True,
                     stop=True,
                 )
-            dst = h_bf[g][s][:, PACK * BLOCK * b : PACK * BLOCK * (b + 1)].rearrange("p (n t) -> p n t", t=PACK)
-            src = bank[:].rearrange("p t n -> p n t")
-            if engine == "S":
-                nc.scalar.activation(dst, src, RELU)
-            else:
-                nc.vector.tensor_scalar_max(dst, src, 0.0)
+            dst = h_bf[g][s][:, PACK * BLOCK * b : PACK * BLOCK * (b + 1)]
+            nc.scalar.activation(
+                dst.rearrange("p (n t) -> p n t", t=PACK), bank[:].rearrange("p t n -> p n t"), RELU
+            )
 
         def quantise_h(g, s):
-            cols = slice(PIECE * s, PIECE * (s + 1))
-            quantise(h_codes[g][:, cols], h_scales[g][:, cols], h_bf[g][s][:])
+            entries = slice(PIECE * s, PIECE * (s + 1))
+            quantise(h_codes[g][:, entries], h_scales[g][:, entries], h_bf[g][s][:])
 
-        def layer2(m, lo, hi, engine):
+        def layer2(engine, m, lo, hi):
             bank = psum.tile([P, hi - lo], F32, name="bank")
             rows = slice(P * m, P * (m + 1))
-            for g in range(2):
+            for g in range(HALVES):
                 nc.tensor.matmul_mx(
                     out=bank[:],
                     lhsT=w2_codes[g][:, rows].bitcast(FP8X4),
@@ -149,61 +157,60 @@ def tile_picked_pick_mlp_relu_srt_e_kernel(tc, xT, w1, w2, offs, out):
                     rhs=h_codes[g][:, lo:hi].bitcast(FP8X4),
                     rhs_scale=h_scales[g][:, lo:hi],
                     start=(g == 0),
-                    stop=(g == 1),
+                    stop=(g == HALVES - 1),
                 )
             result = held.tile([P, hi - lo], F32, name=f"result{m}_{lo}")
             copy(engine, result[:], bank[:])
             nc.sync.dma_start(out[rows, lo:hi], result[:])
 
-        cast_w1("V", 0, 0, 96)
         gather_plane(0)
         gather_plane(1)
         gather_plane(2)
-        gather_last(1)
-        cast_w1("S", 0, 96, 128)
-        cast_w1("S", 1, 80, 128)
-        gather_last(0)
-        cast_x("V", 0, 0, 160)
-        cast_x("S", 1, 0, 256)
-        cast_x("S", 0, 160, 256)
-        quantise_x(0)
-        quantise_w1(0, 256, 512)
+        gather_last_plane(0)
+        gather_last_plane(1)
+        interleave_x("vector", 1, 0, 192)
+        interleave_x("scalar", 0, 0, 256)
+        interleave_x("scalar", 1, 192, 256)
+        gather_last_plane(2)
+        interleave_w1("scalar", 0, 112, 128)
+        interleave_w1("vector", 0, 0, 112)
         quantise_w1(0, 0, 256)
-        gather_last(2)
-        cast_x("V", 2, 0, 256)
-        layer1(0, 0, 0, "S")
-        quantise_x(2)
+        quantise_w1(0, 256, 512)
+        quantise_x(0)
+        interleave_x("scalar", 2, 0, 256)
         quantise_x(1)
-        layer1(0, 1, 0, "S")
-        layer1(0, 2, 1, "V")
-        cast_w1("V", 1, 0, 80)
+        layer1(0, 0, 0)
+        layer1(0, 1, 0)
+        interleave_w1("vector", 1, 0, 128)
         quantise_w1(1, 0, 512)
-        layer1(1, 0, 0, "S")
-        layer1(0, 0, 1, "S")
-        layer1(1, 1, 1, "S")
-        quantise_h(0, 0)
-        layer1(1, 0, 1, "S")
-        layer1(1, 1, 0, "S")
-        layer1(0, 1, 1, "S")
-        layer1(1, 2, 1, "S")
+        layer1(1, 0, 0)
+        layer1(1, 0, 1)
+        layer1(0, 0, 1)
+        quantise_x(2)
+        layer1(1, 1, 0)
+        interleave_w2("vector", 0, 0, 512)
+        layer1(1, 1, 1)
+        layer1(0, 1, 1)
         quantise_h(0, 1)
-        quantise_h(1, 0)
-        cast_w2("V", 0, 0, 512)
+        quantise_h(0, 0)
+        interleave_w2("scalar", 1, 320, 512)
+        layer1(0, 2, 0)
+        layer1(1, 2, 0)
         quantise_w2(0, 0, 512)
-        layer1(1, 2, 0, "S")
-        cast_w2("V", 1, 0, 256)
-        layer1(0, 2, 0, "S")
-        quantise_w2(1, 0, 256)
-        quantise_h(0, 2)
+        layer1(0, 2, 1)
+        interleave_w2("vector", 1, 0, 320)
         quantise_h(1, 1)
-        layer2(0, 0, 512, "S")
-        cast_w2("V", 1, 256, 512)
-        layer2(1, 0, 512, "S")
+        quantise_w2(1, 0, 256)
         quantise_w2(1, 256, 512)
+        layer1(1, 2, 1)
+        quantise_h(1, 0)
+        layer2("vector", 0, 0, WIDE)
+        layer2("vector", 1, 0, WIDE)
+        quantise_h(0, 2)
+        layer2("scalar", 2, 0, WIDE)
+        layer2("scalar", 3, 0, WIDE)
         quantise_h(1, 2)
-        layer2(2, 0, 512, "V")
-        layer2(3, 0, 512, "S")
-        layer2(0, 512, 768, "V")
-        layer2(1, 512, 768, "S")
-        layer2(2, 512, 768, "V")
-        layer2(3, 512, 768, "S")
+        layer2("vector", 0, WIDE, S)
+        layer2("scalar", 1, WIDE, S)
+        layer2("vector", 2, WIDE, S)
+        layer2("scalar", 3, WIDE, S)

from contextlib import ExitStack

import concourse.mybir as mybir

K, T, S, H, N = 512, 2048, 768, 1024, 512
FLOPS = 2 * S * K * H + 2 * S * H * N

P = 128
PACK = 4
HALF = P * PACK
HALVES = H // HALF
PIECE = 256
PIECES = S // PIECE
BLOCK = 128
WIDE = 2 * PIECE

F32 = mybir.dt.float32
BF16 = mybir.dt.bfloat16
U32 = mybir.dt.uint32
U16 = mybir.dt.uint16
U8 = mybir.dt.uint8
FP8X4 = mybir.dt.float8_e4m3fn_x4
RELU = mybir.ActivationFunctionType.Relu


def tile_picked_pick_mlp_relu_srt_e_kernel(tc, xT, w1, w2, offs, out):
    nc = tc.nc
    with ExitStack() as ctx:
        held = ctx.enter_context(tc.tile_pool(name="held", bufs=1))
        psum = ctx.enter_context(tc.psum_pool(name="psum", bufs=8))

        def words(width, name):
            return held.tile([P, width], U32, name=name, align_bytes=64)

        def scale_bytes(width, name):
            return held.tile([P, width], U8, name=name, align_bytes=64)

        def bf16_values(width, name):
            return held.tile([P, PACK * width], BF16, name=name, align_bytes=64)

        offsets = held.tile([P, S // 16], U16, name="offsets")
        planes = [held.tile([P, T], F32, name=f"plane{j}", align_bytes=64) for j in range(PACK)]
        picked = held.tile([P, PACK, S], F32, name="picked", align_bytes=64)
        raw_w1 = [held.tile([P, PACK, HALF], F32, name=f"raw_w1_{g}") for g in range(HALVES)]
        raw_w2 = [held.tile([P, PACK, N], F32, name=f"raw_w2_{g}") for g in range(HALVES)]
        x_bf = [bf16_values(PIECE, f"x_bf{s}") for s in range(PIECES)]
        x_codes = [words(PIECE, f"x_codes{s}") for s in range(PIECES)]
        x_scales = [scale_bytes(PIECE, f"x_scales{s}") for s in range(PIECES)]
        w1_bf = [bf16_values(HALF, f"w1_bf{g}") for g in range(HALVES)]
        w1_codes = [words(HALF, f"w1_codes{g}") for g in range(HALVES)]
        w1_scales = [scale_bytes(HALF, f"w1_scales{g}") for g in range(HALVES)]
        w2_bf = [bf16_values(N, f"w2_bf{g}") for g in range(HALVES)]
        w2_codes = [words(N, f"w2_codes{g}") for g in range(HALVES)]
        w2_scales = [scale_bytes(N, f"w2_scales{g}") for g in range(HALVES)]
        h_bf = [[bf16_values(PIECE, f"h_bf{g}{s}") for s in range(PIECES)] for g in range(HALVES)]
        h_codes = [words(S, f"h_codes{g}") for g in range(HALVES)]
        h_scales = [scale_bytes(S, f"h_scales{g}") for g in range(HALVES)]

        x_rows = xT.rearrange("(p j) w -> p j w", j=PACK)
        w1_rows = w1.rearrange("(p j) i -> p j i", j=PACK)
        w2_rows = w2.rearrange("(g p j) m -> g p j m", g=HALVES, j=PACK)
        first_part = T - S + PIECE
        nc.sync.dma_start(planes[0][:], x_rows[:, 0, :])
        nc.sync.dma_start(offsets[:], offs)
        nc.sync.dma_start(planes[1][:], x_rows[:, 1, :])
        nc.sync.dma_start(planes[2][:], x_rows[:, 2, :])
        nc.sync.dma_start(planes[3][:, :first_part], x_rows[:, 3, :first_part])
        nc.sync.dma_start(planes[3][:, first_part:], x_rows[:, 3, first_part:])
        for g in range(HALVES):
            nc.sync.dma_start(raw_w1[g][:], w1_rows[:, :, HALF * g : HALF * (g + 1)])
        for g in range(HALVES):
            nc.sync.dma_start(raw_w2[g][:], w2_rows[g])

        warm_in = held.tile([P, 1], F32, name="warm_in")
        warm_out = held.tile([P, 1], F32, name="warm_out")
        nc.vector.memset(warm_in[:], 0.0)
        nc.scalar.activation(warm_out[:], warm_in[:], RELU)

        def copy(engine, dst, src):
            if engine == "scalar":
                nc.scalar.copy(dst, src)
            else:
                nc.vector.tensor_copy(dst, src)

        def quantise(codes, scales, values):
            nc.vector.quantize_mx(out=codes.bitcast(FP8X4), scales=scales, in_=values)

        def gather_plane(j):
            nc.vector.tensor_copy(picked[:, j, :], planes[j][:].indirect(offsets[:]))

        def gather_last_plane(s):
            entries = slice(PIECE * s, PIECE * (s + 1))
            window = T - S + PIECE * (s + 1)
            nc.vector.tensor_copy(
                picked[:, PACK - 1, entries],
                planes[PACK - 1][:, :window].indirect(offsets[:, PIECE * s // 16 : PIECE * (s + 1) // 16]),
            )

        def interleave(engine, dst, src):
            copy(
                engine,
                dst.rearrange("p (q c j) -> p q j c", c=4, j=PACK),
                src.rearrange("p j (q c) -> p q j c", c=4),
            )

        def interleave_x(engine, s, lo, hi):
            interleave(engine, x_bf[s][:, PACK * lo : PACK * hi], picked[:, :, PIECE * s + lo : PIECE * s + hi])

        def quantise_x(s):
            quantise(x_codes[s][:], x_scales[s][:], x_bf[s][:])

        def interleave_w1(engine, g, lo, hi):
            dst = w1_bf[g][:].rearrange("p (t m j) -> p m j t", t=PACK, j=PACK)
            src = raw_w1[g][:].rearrange("p j (m t) -> p m j t", t=PACK)
            copy(engine, dst[:, lo:hi], src[:, lo:hi])

        def quantise_w1(g, lo, hi):
            quantise(w1_codes[g][:, lo:hi], w1_scales[g][:, lo:hi], w1_bf[g][:, PACK * lo : PACK * hi])

        def interleave_w2(engine, g, lo, hi):
            interleave(engine, w2_bf[g][:, PACK * lo : PACK * hi], raw_w2[g][:, :, lo:hi])

        def quantise_w2(g, lo, hi):
            quantise(w2_codes[g][:, lo:hi], w2_scales[g][:, lo:hi], w2_bf[g][:, PACK * lo : PACK * hi])

        def layer1(g, s, b):
            bank = psum.tile([P, PACK, BLOCK], F32, name="bank")
            tokens = slice(BLOCK * b, BLOCK * (b + 1))
            for t in range(PACK):
                channels = slice(P * t, P * (t + 1))
                nc.tensor.matmul_mx(
                    out=bank[:, t, :],
                    lhsT=w1_codes[g][:, channels].bitcast(FP8X4),
                    lhsT_scale=w1_scales[g][:, channels],
                    rhs=x_codes[s][:, tokens].bitcast(FP8X4),
                    rhs_scale=x_scales[s][:, tokens],
                    start=True,
                    stop=True,
                )
            dst = h_bf[g][s][:, PACK * BLOCK * b : PACK * BLOCK * (b + 1)]
            nc.scalar.activation(
                dst.rearrange("p (n t) -> p n t", t=PACK), bank[:].rearrange("p t n -> p n t"), RELU
            )

        def quantise_h(g, s):
            entries = slice(PIECE * s, PIECE * (s + 1))
            quantise(h_codes[g][:, entries], h_scales[g][:, entries], h_bf[g][s][:])

        def layer2(engine, m, lo, hi):
            bank = psum.tile([P, hi - lo], F32, name="bank")
            rows = slice(P * m, P * (m + 1))
            for g in range(HALVES):
                nc.tensor.matmul_mx(
                    out=bank[:],
                    lhsT=w2_codes[g][:, rows].bitcast(FP8X4),
                    lhsT_scale=w2_scales[g][:, rows],
                    rhs=h_codes[g][:, lo:hi].bitcast(FP8X4),
                    rhs_scale=h_scales[g][:, lo:hi],
                    start=(g == 0),
                    stop=(g == HALVES - 1),
                )
            result = held.tile([P, hi - lo], F32, name=f"result{m}_{lo}")
            copy(engine, result[:], bank[:])
            nc.sync.dma_start(out[rows, lo:hi], result[:])

        gather_plane(0)
        gather_plane(1)
        gather_plane(2)
        gather_last_plane(0)
        gather_last_plane(1)
        interleave_x("vector", 1, 0, 192)
        interleave_x("scalar", 0, 0, 256)
        interleave_x("scalar", 1, 192, 256)
        gather_last_plane(2)
        interleave_w1("scalar", 0, 112, 128)
        interleave_w1("vector", 0, 0, 112)
        quantise_w1(0, 0, 256)
        quantise_w1(0, 256, 512)
        quantise_x(0)
        interleave_x("scalar", 2, 0, 256)
        quantise_x(1)
        layer1(0, 0, 0)
        layer1(0, 1, 0)
        interleave_w1("vector", 1, 0, 128)
        quantise_w1(1, 0, 512)
        layer1(1, 0, 0)
        layer1(1, 0, 1)
        layer1(0, 0, 1)
        quantise_x(2)
        layer1(1, 1, 0)
        interleave_w2("vector", 0, 0, 512)
        layer1(1, 1, 1)
        layer1(0, 1, 1)
        quantise_h(0, 1)
        quantise_h(0, 0)
        interleave_w2("scalar", 1, 320, 512)
        layer1(0, 2, 0)
        layer1(1, 2, 0)
        quantise_w2(0, 0, 512)
        layer1(0, 2, 1)
        interleave_w2("vector", 1, 0, 320)
        quantise_h(1, 1)
        quantise_w2(1, 0, 256)
        quantise_w2(1, 256, 512)
        layer1(1, 2, 1)
        quantise_h(1, 0)
        layer2("vector", 0, 0, WIDE)
        layer2("vector", 1, 0, WIDE)
        quantise_h(0, 2)
        layer2("scalar", 2, 0, WIDE)
        layer2("scalar", 3, 0, WIDE)
        quantise_h(1, 2)
        layer2("vector", 0, WIDE, S)
        layer2("scalar", 1, WIDE, S)
        layer2("vector", 2, WIDE, S)
        layer2("scalar", 3, WIDE, S)
